import numpy as np
import ml_dtypes


def mxq(x, axis, fmt="e4m3"):
    dtype, down = {"e4m3": (ml_dtypes.float8_e4m3fn, 7), "e5m2": (ml_dtypes.float8_e5m2, 14)}[fmt]
    v = np.moveaxis(np.asarray(x, np.float32).astype(ml_dtypes.bfloat16).astype(np.float64), axis, -1)
    blocks = v.reshape(v.shape[:-1] + (-1, 32))
    amax = np.abs(blocks).max(-1, keepdims=True)
    byte = np.maximum(np.where(amax > 0, np.frexp(amax)[1] - 1 + 127, 0) - down, 1)
    scale = np.exp2(byte - 127.0)
    codes = (blocks / scale).astype(np.float32).astype(dtype).astype(np.float64)
    return np.moveaxis((codes * scale).reshape(v.shape), -1, axis)


WIDE = False


def mx_kscale(k):
    if not WIDE:
        return np.ones(k)
    levels = np.array([24, -24, 12, -12, 0])
    if k % 512:
        return np.exp2(np.random.permutation(np.resize(levels, k // 32))).repeat(32)
    a = np.empty((k // 512, 16))
    for p in range(k // 512):
        a[p, :8] = np.random.permutation(np.resize(levels, 8))
        for g in range(8):
            far = levels[np.abs(levels - a[p, g]) >= 10]
            a[p, g + 8] = far[np.random.randint(len(far))]
    return np.exp2(a.ravel()).repeat(32)


def f64(x):
    return np.asarray(x).astype(np.float64)


def striped8(idx):
    return np.concatenate([v.reshape(-1, 16).T for v in idx]).astype(np.uint16)


def unstriped8(offs):
    return np.stack([offs[16 * g:16 * g + 16].T.reshape(-1) for g in range(8)]).astype(np.int64)


def planes(y):
    n, m = y.shape
    v = y.astype(np.float32).astype(ml_dtypes.bfloat16).astype(np.float64).reshape(n // 32, 32, m)
    top = np.abs(v).max(1)
    byte = np.clip(np.where(top > 0, np.frexp(top)[1] - 1 + 127 - 7, 1), 1, 254)
    codes = (v * np.exp2(127.0 - byte)[:, None, :]).reshape(n, m).astype(np.float32).astype(ml_dtypes.float8_e4m3fn).view(np.uint8)
    words = codes.reshape(n // 512, 128, 4, m).transpose(0, 1, 3, 2)
    return np.ascontiguousarray(words), np.ascontiguousarray(byte.astype(np.uint8).reshape(n // 512, 16, m))


def silu(f):
    return f / (1.0 + np.exp(-np.maximum(f, -700.0)))


K, R, N, T, J = 1024, 1024, 512, 2048, 1024


def setup_inputs():
    n = np.random.standard_normal
    s = mx_kscale(K)[:, None]
    u = mx_kscale(R)[:, None]
    return {
        "xT": (n((K, T)) * s).astype(np.float32),
        "wgt": np.repeat(np.random.uniform(0.5, 2.0, (8, J)), 16, axis=0).astype(np.float32),
        "wg": (n((K, R)) / np.sqrt(K) / s).astype(np.float32),
        "wu": (n((K, R)) / np.sqrt(K) / s * u.T).astype(np.float32),
        "wd": (n((R, N)) / np.sqrt(R) / u).astype(np.float32),
        "offs": striped8(np.stack([np.random.permutation(T)[:J] for _ in range(8)])),
    }


def reference(xT, wgt, wg, wu, wd, offs):
    idx = unstriped8(offs)
    rows = np.arange(K)
    xg = f64(wgt)[rows // 4 % 128] * f64(xT)[rows[:, None], idx[rows % 512 // 64]]
    xT_ = mxq(xg, 0, "e4m3")
    wg_ = mxq(f64(wg), 0, "e4m3")
    wu_ = mxq(f64(wu), 0, "e4m3")
    ga = wg_.T @ xT_
    ub = wu_.T @ xT_
    h = silu(ga) * ub
    h_ = mxq(h, 0, "e4m3")
    wd_ = mxq(f64(wd), 0, "e4m3")
    y = wd_.T @ h_
    return (y,) + planes(y)

@@ -1,0 +1,262 @@
+from contextlib import ExitStack
+
+import concourse.mybir as mybir
+
+K, R, N, T, J = 1024, 1024, 512, 2048, 1024
+FLOPS = 2 * (2 * K * R * J + R * N * J)
+
+F32 = mybir.dt.float32
+BF16 = mybir.dt.bfloat16
+I32 = mybir.dt.int32
+U32 = mybir.dt.uint32
+U16 = mybir.dt.uint16
+U8 = mybir.dt.uint8
+FP8X4 = mybir.dt.float8_e4m3fn_x4
+MULT = mybir.AluOpType.mult
+SILU = mybir.ActivationFunctionType.Silu
+
+P = 128
+PACK = 4
+PASS = P * PACK
+HALF = J // 2
+QUARTER = J // 4
+CHUNK = 128
+LIST_ROWS = 16
+
+
+def tile_list_silu_noneP_kernel(
+    tc, xT, wgt, wg, wu, wd, offs, out_0, out_1, out_2
+):
+    nc = tc.nc
+    with ExitStack() as ctx:
+        keep = ctx.enter_context(tc.tile_pool(name="keep", bufs=1))
+        raw = ctx.enter_context(tc.tile_pool(name="raw", bufs=12))
+        stage = ctx.enter_context(tc.tile_pool(name="stage", bufs=3))
+        acts = ctx.enter_context(tc.tile_pool(name="acts", bufs=8))
+        psum = ctx.enter_context(tc.psum_pool(name="psum", bufs=8))
+
+        offsets = keep.tile([P, J // LIST_ROWS], U16, name="offsets")
+        nc.sync.dma_start(offsets[:], offs)
+
+        x_rows = xT.rearrange("(a p i) t -> a i p t", p=P, i=PACK)
+        planes = {}
+        gains = {}
+        weights = {}
+
+        def load_plane(n):
+            planes[n] = raw.tile([P, T], F32, name="plane%d" % n, tag="raw")
+            nc.sync.dma_start(planes[n][:], x_rows[n // PACK, n % PACK])
+
+        def load_gain(h):
+            gains[h] = keep.tile([P, HALF], F32, name="gain%d" % h)
+            nc.sync.dma_start(gains[h][:], wgt[:, h * HALF : (h + 1) * HALF])
+
+        def load_weight(key, w, a, b):
+            weights[key] = raw.tile([P, PACK, PASS], F32, name="w_%s" % key, tag="raw")
+            rows = w[a * PASS : (a + 1) * PASS, b * PASS : (b + 1) * PASS]
+            nc.sync.dma_start(weights[key][:], rows.rearrange("(p i) c -> p i c", i=PACK))
+
+        load_plane(0)
+        load_gain(0)
+        load_gain(1)
+        for n in range(1, 5):
+            load_plane(n)
+        load_weight("g00", wg, 0, 0)
+        for n in range(5, 8):
+            load_plane(n)
+        load_weight("g10", wg, 1, 0)
+        for name, w, b in (("u", wu, 0), ("g", wg, 1), ("u", wu, 1), ("d", wd, 0)):
+            for a in range(2):
+                load_weight("%s%d%d" % (name, a, b), w, a, b)
+
+        picked = {}
+        for a in range(2):
+            for h in range(2):
+                picked[a, h] = keep.tile([P, PACK, HALF], F32, name="picked%d%d" % (a, h))
+
+        def gather(n, j0, width):
+            a, i = divmod(n, PACK)
+            h, c0 = divmod(j0, HALF)
+            nc.vector.tensor_tensor(
+                picked[a, h][:, i, c0 : c0 + width],
+                planes[n][:].indirect(offsets[:, j0 // LIST_ROWS : (j0 + width) // LIST_ROWS]),
+                gains[h][:, c0 : c0 + width],
+                MULT,
+            )
+
+        def quantize(src, width, name):
+            codes = keep.tile([P, width], U32, name="c_" + name, align_bytes=64)
+            scales = keep.tile([P, width], U8, name="s_" + name, align_bytes=64)
+            nc.vector.quantize_mx(out=codes[:].bitcast(FP8X4), scales=scales[:], in_=src)
+            return codes, scales
+
+        def copy_on(engine, out, in_):
+            if engine == "scalar":
+                nc.scalar.copy(out, in_)
+            else:
+                nc.vector.tensor_copy(out, in_)
+
+        rounded = {}
+        wq = {}
+        xq = {}
+        hq = {}
+
+        def round_weight(key, engine):
+            rounded[key] = stage.tile([P, PACK * PASS], BF16, name="r_" + key, tag="wbf", align_bytes=64)
+            copy_on(
+                engine,
+                rounded[key][:].rearrange("p (t m i) -> p m i t", t=PACK, i=PACK),
+                weights[key][:].rearrange("p i (m t) -> p m i t", t=PACK),
+            )
+
+        def quantize_weight(key):
+            wq[key] = quantize(rounded[key][:], PASS, key)
+
+        def round_picked(a, j0, width):
+            h, c0 = divmod(j0, HALF)
+            rounded[a, j0] = stage.tile([P, PACK * width], BF16, name="rx%d_%d" % (a, j0), tag="xbf", align_bytes=64)
+            nc.scalar.copy(
+                rounded[a, j0][:].rearrange("p (c e i) -> p c i e", e=4, i=PACK),
+                picked[a, h][:, :, c0 : c0 + width].rearrange("p i (c e) -> p c i e", e=4),
+            )
+
+        def quantize_picked(a, j0, width):
+            pair = quantize(rounded[a, j0][:], width, "x%d_%d" % (a, j0))
+            for c0 in range(0, width, CHUNK):
+                xq[a, (j0 + c0) // CHUNK] = (pair[0][:, c0 : c0 + CHUNK], pair[1][:, c0 : c0 + CHUNK])
+
+        def product(stationary, moving):
+            bank = psum.tile([P, PACK, CHUNK], F32, name="bank")
+            for a in range(2):
+                for t in range(PACK):
+                    cols = slice(t * P, (t + 1) * P)
+                    nc.tensor.matmul_mx(
+                        out=bank[:, t, :],
+                        lhsT=stationary[a][0][:, cols].bitcast(FP8X4),
+                        lhsT_scale=stationary[a][1][:, cols],
+                        rhs=moving[a][0].bitcast(FP8X4),
+                        rhs_scale=moving[a][1],
+                        start=(a == 0 and t == 0),
+                        stop=(a == 1 and t == PACK - 1),
+                    )
+            return bank
+
+        warm = keep.tile([P, 1], F32, name="warm")
+        nc.vector.memset(warm[:], 0.0)
+        warm2 = keep.tile([P, 1], F32, name="warm2")
+        nc.scalar.activation(warm2[:], warm[:], SILU)
+
+        for n in range(4):
+            for h in range(2):
+                gather(n, h * HALF, HALF)
+        round_picked(0, 0, HALF)
+        round_picked(0, HALF, HALF)
+        round_weight("g00", "scalar")
+        gather(4, 0, HALF)
+        gather(4, HALF, HALF)
+        quantize_picked(0, 0, HALF)
+        gather(5, 0, HALF)
+        gather(5, HALF, HALF)
+        quantize_picked(0, HALF, HALF)
+        gather(6, 0, HALF)
+        quantize_weight("g00")
+        gather(6, HALF, HALF)
+        for q in range(4):
+            gather(7, q * QUARTER, QUARTER)
+            round_picked(1, q * QUARTER, QUARTER)
+        round_weight("g10", "vector")
+        quantize_picked(1, 0, QUARTER)
+        quantize_weight("g10")
+        for q in range(1, 4):
+            quantize_picked(1, q * QUARTER, QUARTER)
+
+        chunks = J // CHUNK
+        gates = {}
+
+        def gate(b, c):
+            bank = product([wq["g0%d" % b], wq["g1%d" % b]], [xq[0, c], xq[1, c]])
+            gates[b, c] = acts.tile([P, CHUNK, PACK], F32, name="gate%d_%d" % (b, c), tag="gate")
+            nc.scalar.activation(gates[b, c][:], bank[:].rearrange("p t j -> p j t"), SILU)
+
+        hidden = {}
+
+        def up(b, c):
+            bank = product([wq["u0%d" % b], wq["u1%d" % b]], [xq[0, c], xq[1, c]])
+            hidden[b, c] = acts.tile([P, CHUNK, PACK], BF16, name="h%d_%d" % (b, c), tag="hid", align_bytes=64)
+            nc.vector.tensor_tensor(hidden[b, c][:], bank[:].rearrange("p t j -> p j t"), gates[b, c][:], MULT)
+
+        def quantize_hidden(b, c):
+            pair = quantize(hidden[b, c][:].rearrange("p j t -> p (j t)"), CHUNK, "h%d_%d" % (b, c))
+            hq[b, c] = (pair[0][:], pair[1][:])
+
+        def ups(b):
+            for c in range(chunks + 1):
+                if c < chunks:
+                    up(b, c)
+                if c > 0:
+                    quantize_hidden(b, c - 1)
+
+
+        y_rows = out_0.rearrange("(p t) j -> p t j", t=PACK)
+        words = out_1[0].rearrange("p j i -> p (j i)").bitcast(I32)
+        y_codes = keep.tile([P, J], U32, name="y_codes", align_bytes=64)
+        y_scales = keep.tile([P, J], U8, name="y_scales", align_bytes=64)
+        ys = {}
+        yb = {}
+
+        def down(c):
+            q, half = divmod(c, 2)
+            if half == 0:
+                ys[q] = raw.tile([P, PACK, QUARTER], F32, name="y%d" % q, tag="raw")
+            bank = product([wq["d00"], wq["d10"]], [hq[0, c], hq[1, c]])
+            nc.scalar.copy(ys[q][:, :, half * CHUNK : (half + 1) * CHUNK], bank[:])
+
+        def round_y(q):
+            cols = slice(q * QUARTER, (q + 1) * QUARTER)
+            nc.sync.dma_start(y_rows[:, :, cols], ys[q][:])
+            yb[q] = stage.tile([P, PACK * QUARTER], BF16, name="yb%d" % q, tag="xbf", align_bytes=64)
+            nc.vector.tensor_copy(
+                yb[q][:].rearrange("p (c e t) -> p c t e", e=4, t=PACK),
+                ys[q][:].rearrange("p t (c e) -> p c t e", e=4),
+            )
+
+        def quantize_y(q):
+            cols = slice(q * QUARTER, (q + 1) * QUARTER)
+            nc.vector.quantize_mx(out=y_codes[:, cols].bitcast(FP8X4), scales=y_scales[:, cols], in_=yb[q][:])
+            nc.sync.dma_start(words[:, cols], y_codes[:, cols].bitcast(I32))
+
+        round_weight("u00", "vector")
+        quantize_weight("u00")
+        for c in range(chunks):
+            gate(0, c)
+        round_weight("u10", "vector")
+        quantize_weight("u10")
+        round_weight("g01", "scalar")
+        round_weight("g11", "scalar")
+        quantize_weight("g01")
+        quantize_weight("g11")
+        ups(0)
+        round_weight("u01", "scalar")
+        round_weight("u11", "vector")
+        quantize_weight("u01")
+        quantize_weight("u11")
+        round_weight("d00", "scalar")
+        quantize_weight("d00")
+        for c in range(chunks):
+            gate(1, c)
+        round_weight("d10", "scalar")
+        quantize_weight("d10")
+        for c in range(chunks + 5):
+            if c < chunks:
+                up(1, c)
+            if 1 <= c <= chunks:
+                quantize_hidden(1, c - 1)
+            if 2 <= c < chunks + 2:
+                down(c - 2)
+            if c >= 4 and c % 2 == 0 and c < chunks + 4:
+                round_y((c - 4) // 2)
+            if c >= 5 and c % 2 == 1:
+                quantize_y((c - 5) // 2)
+        scale_rows = out_2[0].bitcast(I32)
+        for g in range(4):
+            nc.scalar.dma_start(scale_rows[4 * g : 4 * g + 4, :], y_scales[32 * g : 32 * g + 4, :].bitcast(I32))

@@ -21,17 +21,21 @@ PASS = P * PACK
 HALF = J // 2
 QUARTER = J // 4
 CHUNK = 128
+CHUNKS = J // CHUNK
 LIST_ROWS = 16
+H_GROUP = 2
 
 
 def tile_list_silu_noneP_kernel(
     tc, xT, wgt, wg, wu, wd, offs, out_0, out_1, out_2
 ):
     nc = tc.nc
+    scalar_copy = nc.scalar.copy
+    vector_copy = nc.vector.tensor_copy
     with ExitStack() as ctx:
         keep = ctx.enter_context(tc.tile_pool(name="keep", bufs=1))
-        raw = ctx.enter_context(tc.tile_pool(name="raw", bufs=12))
-        stage = ctx.enter_context(tc.tile_pool(name="stage", bufs=3))
+        raw = ctx.enter_context(tc.tile_pool(name="raw", bufs=11))
+        stage = ctx.enter_context(tc.tile_pool(name="stage", bufs=4))
         acts = ctx.enter_context(tc.tile_pool(name="acts", bufs=8))
         psum = ctx.enter_context(tc.psum_pool(name="psum", bufs=8))
 
@@ -40,49 +44,47 @@ def tile_list_silu_noneP_kernel(
 
         x_rows = xT.rearrange("(a p i) t -> a i p t", p=P, i=PACK)
         planes = {}
-        gains = {}
         weights = {}
+        blocks = [
+            (name, w, a, b)
+            for name, w, b in (("g", wg, 0), ("u", wu, 0), ("g", wg, 1), ("u", wu, 1), ("d", wd, 0))
+            for a in range(2)
+        ]
 
         def load_plane(n):
             planes[n] = raw.tile([P, T], F32, name="plane%d" % n, tag="raw")
             nc.sync.dma_start(planes[n][:], x_rows[n // PACK, n % PACK])
 
-        def load_gain(h):
-            gains[h] = keep.tile([P, HALF], F32, name="gain%d" % h)
-            nc.sync.dma_start(gains[h][:], wgt[:, h * HALF : (h + 1) * HALF])
-
-        def load_weight(key, w, a, b):
-            weights[key] = raw.tile([P, PACK, PASS], F32, name="w_%s" % key, tag="raw")
+        def load_weight(name, w, a, b):
+            weights[name, a, b] = raw.tile([P, PACK, PASS], F32, name="w_%s%d%d" % (name, a, b), tag="raw")
             rows = w[a * PASS : (a + 1) * PASS, b * PASS : (b + 1) * PASS]
-            nc.sync.dma_start(weights[key][:], rows.rearrange("(p i) c -> p i c", i=PACK))
+            nc.sync.dma_start(weights[name, a, b][:], rows.rearrange("(p i) c -> p i c", i=PACK))
 
+        gain = keep.tile([P, J], F32, name="gain")
         load_plane(0)
-        load_gain(0)
-        load_gain(1)
-        for n in range(1, 5):
+        for j0 in (0, HALF):
+            nc.sync.dma_start(gain[:, j0 : j0 + HALF], wgt[:, j0 : j0 + HALF])
+        early = 0
+        for n in range(1, 2 * PACK):
             load_plane(n)
-        load_weight("g00", wg, 0, 0)
-        for n in range(5, 8):
-            load_plane(n)
-        load_weight("g10", wg, 1, 0)
-        for name, w, b in (("u", wu, 0), ("g", wg, 1), ("u", wu, 1), ("d", wd, 0)):
-            for a in range(2):
-                load_weight("%s%d%d" % (name, a, b), w, a, b)
+            if n in (2, 4, 6):
+                load_weight(*blocks[early])
+                early = early + 1
+        for block in blocks[early:]:
+            load_weight(*block)
 
+        halves = ((0, HALF), (HALF, HALF))
+        spans = (halves, ((0, QUARTER), (QUARTER, QUARTER), (HALF, HALF)))
         picked = {}
         for a in range(2):
-            for h in range(2):
-                picked[a, h] = keep.tile([P, PACK, HALF], F32, name="picked%d%d" % (a, h))
+            for j0, width in spans[a]:
+                picked[a, j0] = keep.tile([P, PACK, width], F32, name="picked%d_%d" % (a, j0))
 
-        def gather(n, j0, width):
+        def gather(n, base, j0, width):
             a, i = divmod(n, PACK)
-            h, c0 = divmod(j0, HALF)
-            nc.vector.tensor_tensor(
-                picked[a, h][:, i, c0 : c0 + width],
-                planes[n][:].indirect(offsets[:, j0 // LIST_ROWS : (j0 + width) // LIST_ROWS]),
-                gains[h][:, c0 : c0 + width],
-                MULT,
-            )
+            dst = picked[a, base][:, i, j0 - base : j0 - base + width]
+            window = planes[n][:].indirect(offsets[:, j0 // LIST_ROWS : (j0 + width) // LIST_ROWS])
+            nc.vector.tensor_tensor(dst, window, gain[:, j0 : j0 + width], MULT)
 
         def quantize(src, width, name):
             codes = keep.tile([P, width], U32, name="c_" + name, align_bytes=64)
@@ -90,50 +92,46 @@ def tile_list_silu_noneP_kernel(
             nc.vector.quantize_mx(out=codes[:].bitcast(FP8X4), scales=scales[:], in_=src)
             return codes, scales
 
-        def copy_on(engine, out, in_):
-            if engine == "scalar":
-                nc.scalar.copy(out, in_)
-            else:
-                nc.vector.tensor_copy(out, in_)
+        def chunk_of(pair, c0):
+            return pair[0][:, c0 : c0 + CHUNK], pair[1][:, c0 : c0 + CHUNK]
 
         rounded = {}
         wq = {}
         xq = {}
         hq = {}
 
-        def round_weight(key, engine):
-            rounded[key] = stage.tile([P, PACK * PASS], BF16, name="r_" + key, tag="wbf", align_bytes=64)
-            copy_on(
-                engine,
+        def round_weight(key, copy):
+            rounded[key] = stage.tile([P, PACK * PASS], BF16, name="r_%s%d%d" % key, tag="wbf", align_bytes=64)
+            copy(
                 rounded[key][:].rearrange("p (t m i) -> p m i t", t=PACK, i=PACK),
                 weights[key][:].rearrange("p i (m t) -> p m i t", t=PACK),
             )
 
         def quantize_weight(key):
-            wq[key] = quantize(rounded[key][:], PASS, key)
+            wq[key] = quantize(rounded[key][:], PASS, "%s%d%d" % key)
 
-        def round_picked(a, j0, width):
-            h, c0 = divmod(j0, HALF)
-            rounded[a, j0] = stage.tile([P, PACK * width], BF16, name="rx%d_%d" % (a, j0), tag="xbf", align_bytes=64)
+        def round_picked(a, base, j0, width):
+            rounded[a, j0] = stage.tile([P, PACK * width], BF16, name="rx%d_%d" % (a, j0), tag="xbf", bufs=3, align_bytes=64)
             nc.scalar.copy(
                 rounded[a, j0][:].rearrange("p (c e i) -> p c i e", e=4, i=PACK),
-                picked[a, h][:, :, c0 : c0 + width].rearrange("p i (c e) -> p c i e", e=4),
+                picked[a, base][:, :, j0 - base : j0 - base + width].rearrange("p i (c e) -> p c i e", e=4),
             )
 
         def quantize_picked(a, j0, width):
             pair = quantize(rounded[a, j0][:], width, "x%d_%d" % (a, j0))
             for c0 in range(0, width, CHUNK):
-                xq[a, (j0 + c0) // CHUNK] = (pair[0][:, c0 : c0 + CHUNK], pair[1][:, c0 : c0 + CHUNK])
+                xq[a, (j0 + c0) // CHUNK] = chunk_of(pair, c0)
 
-        def product(stationary, moving):
+        def product(name, b, moving):
             bank = psum.tile([P, PACK, CHUNK], F32, name="bank")
             for a in range(2):
+                codes, scales = wq[name, a, b]
                 for t in range(PACK):
                     cols = slice(t * P, (t + 1) * P)
                     nc.tensor.matmul_mx(
                         out=bank[:, t, :],
-                        lhsT=stationary[a][0][:, cols].bitcast(FP8X4),
-                        lhsT_scale=stationary[a][1][:, cols],
+                        lhsT=codes[:, cols].bitcast(FP8X4),
+                        lhsT_scale=scales[:, cols],
                         rhs=moving[a][0].bitcast(FP8X4),
                         rhs_scale=moving[a][1],
                         start=(a == 0 and t == 0),
@@ -141,61 +139,64 @@ def tile_list_silu_noneP_kernel(
                     )
             return bank
 
+        zero = keep.tile([P, 1], F32, name="zero")
+        nc.vector.memset(zero[:], 0.0)
         warm = keep.tile([P, 1], F32, name="warm")
-        nc.vector.memset(warm[:], 0.0)
-        warm2 = keep.tile([P, 1], F32, name="warm2")
-        nc.scalar.activation(warm2[:], warm[:], SILU)
+        nc.scalar.activation(warm[:], zero[:], SILU)
 
-        for n in range(4):
-            for h in range(2):
-                gather(n, h * HALF, HALF)
-        round_picked(0, 0, HALF)
-        round_picked(0, HALF, HALF)
-        round_weight("g00", "scalar")
-        gather(4, 0, HALF)
-        gather(4, HALF, HALF)
-        quantize_picked(0, 0, HALF)
-        gather(5, 0, HALF)
-        gather(5, HALF, HALF)
-        quantize_picked(0, HALF, HALF)
-        gather(6, 0, HALF)
-        quantize_weight("g00")
-        gather(6, HALF, HALF)
-        for q in range(4):
-            gather(7, q * QUARTER, QUARTER)
-            round_picked(1, q * QUARTER, QUARTER)
-        round_weight("g10", "vector")
-        quantize_picked(1, 0, QUARTER)
-        quantize_weight("g10")
-        for q in range(1, 4):
-            quantize_picked(1, q * QUARTER, QUARTER)
+        for n in range(PACK):
+            for j0, width in halves:
+                gather(n, j0, j0, width)
+        for j0, width in halves:
+            round_picked(0, j0, j0, width)
+        round_weight(("g", 0, 0), scalar_copy)
+        round_weight(("g", 1, 0), scalar_copy)
+        round_weight(("u", 0, 0), scalar_copy)
+        for n in range(PACK, 2 * PACK - 1):
+            for j0, width in spans[1]:
+                gather(n, j0, j0, width)
+        for j0, width in halves:
+            quantize_picked(0, j0, width)
+        quantize_weight(("g", 0, 0))
+        quantize_weight(("g", 1, 0))
+        for j0, width in spans[1]:
+            gather(2 * PACK - 1, j0, j0, width)
+            round_picked(1, j0, j0, width)
+        for j0, width in spans[1]:
+            quantize_picked(1, j0, width)
 
-        chunks = J // CHUNK
         gates = {}
+        hidden = {}
 
         def gate(b, c):
-            bank = product([wq["g0%d" % b], wq["g1%d" % b]], [xq[0, c], xq[1, c]])
+            bank = product("g", b, [xq[0, c], xq[1, c]])
             gates[b, c] = acts.tile([P, CHUNK, PACK], F32, name="gate%d_%d" % (b, c), tag="gate")
             nc.scalar.activation(gates[b, c][:], bank[:].rearrange("p t j -> p j t"), SILU)
 
-        hidden = {}
-
         def up(b, c):
-            bank = product([wq["u0%d" % b], wq["u1%d" % b]], [xq[0, c], xq[1, c]])
-            hidden[b, c] = acts.tile([P, CHUNK, PACK], BF16, name="h%d_%d" % (b, c), tag="hid", align_bytes=64)
-            nc.vector.tensor_tensor(hidden[b, c][:], bank[:].rearrange("p t j -> p j t"), gates[b, c][:], MULT)
+            g, s = divmod(c, H_GROUP)
+            bank = product("u", b, [xq[0, c], xq[1, c]])
+            if s == 0:
+                hidden[b, g] = stage.tile(
+                    [P, H_GROUP * PASS], BF16, name="h%d_%d" % (b, g), tag="hid", align_bytes=64
+                )
+            nc.vector.tensor_tensor(
+                hidden[b, g][:, s * PASS : (s + 1) * PASS].rearrange("p (j t) -> p j t", t=PACK),
+                bank[:].rearrange("p t j -> p j t"),
+                gates[b, c][:],
+                MULT,
+            )
 
-        def quantize_hidden(b, c):
-            pair = quantize(hidden[b, c][:].rearrange("p j t -> p (j t)"), CHUNK, "h%d_%d" % (b, c))
-            hq[b, c] = (pair[0][:], pair[1][:])
+        def quantize_hidden(b, g):
+            pair = quantize(hidden[b, g][:], H_GROUP * CHUNK, "h%d_%d" % (b, g))
+            for s in range(H_GROUP):
+                hq[b, g * H_GROUP + s] = chunk_of(pair, s * CHUNK)
 
-        def ups(b):
-            for c in range(chunks + 1):
-                if c < chunks:
-                    up(b, c)
-                if c > 0:
-                    quantize_hidden(b, c - 1)
-
+        def prepare(name, b, first, second):
+            round_weight((name, 0, b), first)
+            round_weight((name, 1, b), second)
+            for a in range(2):
+                quantize_weight((name, a, b))
 
         y_rows = out_0.rearrange("(p t) j -> p t j", t=PACK)
         words = out_1[0].rearrange("p j i -> p (j i)").bitcast(I32)
@@ -208,13 +209,13 @@ def tile_list_silu_noneP_kernel(
             q, half = divmod(c, 2)
             if half == 0:
                 ys[q] = raw.tile([P, PACK, QUARTER], F32, name="y%d" % q, tag="raw")
-            bank = product([wq["d00"], wq["d10"]], [hq[0, c], hq[1, c]])
+            bank = product("d", 0, [hq[0, c], hq[1, c]])
             nc.scalar.copy(ys[q][:, :, half * CHUNK : (half + 1) * CHUNK], bank[:])
 
         def round_y(q):
             cols = slice(q * QUARTER, (q + 1) * QUARTER)
             nc.sync.dma_start(y_rows[:, :, cols], ys[q][:])
-            yb[q] = stage.tile([P, PACK * QUARTER], BF16, name="yb%d" % q, tag="xbf", align_bytes=64)
+            yb[q] = stage.tile([P, PACK * QUARTER], BF16, name="yb%d" % q, tag="xbf", bufs=3, align_bytes=64)
             nc.vector.tensor_copy(
                 yb[q][:].rearrange("p (c e t) -> p c t e", e=4, t=PACK),
                 ys[q][:].rearrange("p t (c e) -> p c t e", e=4),
@@ -225,38 +226,35 @@ def tile_list_silu_noneP_kernel(
             nc.vector.quantize_mx(out=y_codes[:, cols].bitcast(FP8X4), scales=y_scales[:, cols], in_=yb[q][:])
             nc.sync.dma_start(words[:, cols], y_codes[:, cols].bitcast(I32))
 
-        round_weight("u00", "vector")
-        quantize_weight("u00")
-        for c in range(chunks):
+        round_weight(("u", 1, 0), vector_copy)
+        for a in range(2):
+            quantize_weight(("u", a, 0))
+        for c in range(CHUNKS):
             gate(0, c)
-        round_weight("u10", "vector")
-        quantize_weight("u10")
-        round_weight("g01", "scalar")
-        round_weight("g11", "scalar")
-        quantize_weight("g01")
-        quantize_weight("g11")
-        ups(0)
-        round_weight("u01", "scalar")
-        round_weight("u11", "vector")
-        quantize_weight("u01")
-        quantize_weight("u11")
-        round_weight("d00", "scalar")
-        quantize_weight("d00")
-        for c in range(chunks):
+        prepare("g", 1, scalar_copy, vector_copy)
+        for c in range(CHUNKS + 1):
+            if c < CHUNKS:
+                up(0, c)
+            if c > 0 and c % H_GROUP == 0:
+                quantize_hidden(0, c // H_GROUP - 1)
+        prepare("u", 1, scalar_copy, vector_copy)
+        prepare("d", 0, scalar_copy, vector_copy)
+        for c in range(CHUNKS):
             gate(1, c)
-        round_weight("d10", "scalar")
-        quantize_weight("d10")
-        for c in range(chunks + 5):
-            if c < chunks:
-                up(1, c)
-            if 1 <= c <= chunks:
-                quantize_hidden(1, c - 1)
-            if 2 <= c < chunks + 2:
-                down(c - 2)
-            if c >= 4 and c % 2 == 0 and c < chunks + 4:
-                round_y((c - 4) // 2)
-            if c >= 5 and c % 2 == 1:
-                quantize_y((c - 5) // 2)
+        for q in range(4 + 3):
+            if q < 4:
+                up(1, 2 * q)
+            if 1 <= q < 5:
+                for g in range(2 // H_GROUP):
+                    quantize_hidden(1, (q - 1) * (2 // H_GROUP) + g)
+                down(2 * q - 2)
+                down(2 * q - 1)
+            if q < 4:
+                up(1, 2 * q + 1)
+            if 2 <= q < 6:
+                round_y(q - 2)
+            if 3 <= q:
+                quantize_y(q - 3)
         scale_rows = out_2[0].bitcast(I32)
         for g in range(4):
             nc.scalar.dma_start(scale_rows[4 * g : 4 * g + 4, :], y_scales[32 * g : 32 * g + 4, :].bitcast(I32))

@@ -34,9 +34,9 @@ def tile_list_silu_noneP_kernel(
     vector_copy = nc.vector.tensor_copy
     with ExitStack() as ctx:
         keep = ctx.enter_context(tc.tile_pool(name="keep", bufs=1))
-        raw = ctx.enter_context(tc.tile_pool(name="raw", bufs=11))
+        raw = ctx.enter_context(tc.tile_pool(name="raw", bufs=9))
         stage = ctx.enter_context(tc.tile_pool(name="stage", bufs=4))
-        acts = ctx.enter_context(tc.tile_pool(name="acts", bufs=8))
+        acts = ctx.enter_context(tc.tile_pool(name="acts", bufs=16))
         psum = ctx.enter_context(tc.psum_pool(name="psum", bufs=8))
 
         offsets = keep.tile([P, J // LIST_ROWS], U16, name="offsets")
@@ -45,11 +45,8 @@ def tile_list_silu_noneP_kernel(
         x_rows = xT.rearrange("(a p i) t -> a i p t", p=P, i=PACK)
         planes = {}
         weights = {}
-        blocks = [
-            (name, w, a, b)
-            for name, w, b in (("g", wg, 0), ("u", wu, 0), ("g", wg, 1), ("u", wu, 1), ("d", wd, 0))
-            for a in range(2)
-        ]
+        blocks = [(name, w, a, b) for name, w in (("g", wg), ("u", wu)) for a in range(2) for b in range(2)]
+        blocks = blocks + [("d", wd, a, 0) for a in range(2)]
 
         def load_plane(n):
             planes[n] = raw.tile([P, T], F32, name="plane%d" % n, tag="raw")
@@ -67,7 +64,7 @@ def tile_list_silu_noneP_kernel(
         early = 0
         for n in range(1, 2 * PACK):
             load_plane(n)
-            if n in (2, 4, 6):
+            if n in (4, 5, 6):
                 load_weight(*blocks[early])
                 early = early + 1
         for block in blocks[early:]:
@@ -150,14 +147,15 @@ def tile_list_silu_noneP_kernel(
         for j0, width in halves:
             round_picked(0, j0, j0, width)
         round_weight(("g", 0, 0), scalar_copy)
+        round_weight(("g", 0, 1), scalar_copy)
         round_weight(("g", 1, 0), scalar_copy)
-        round_weight(("u", 0, 0), scalar_copy)
         for n in range(PACK, 2 * PACK - 1):
             for j0, width in spans[1]:
                 gather(n, j0, j0, width)
         for j0, width in halves:
             quantize_picked(0, j0, width)
         quantize_weight(("g", 0, 0))
+        quantize_weight(("g", 0, 1))
         quantize_weight(("g", 1, 0))
         for j0, width in spans[1]:
             gather(2 * PACK - 1, j0, j0, width)
@@ -174,23 +172,20 @@ def tile_list_silu_noneP_kernel(
             nc.scalar.activation(gates[b, c][:], bank[:].rearrange("p t j -> p j t"), SILU)
 
         def up(b, c):
-            g, s = divmod(c, H_GROUP)
             bank = product("u", b, [xq[0, c], xq[1, c]])
-            if s == 0:
-                hidden[b, g] = stage.tile(
-                    [P, H_GROUP * PASS], BF16, name="h%d_%d" % (b, g), tag="hid", align_bytes=64
-                )
+            if b == 0:
+                hidden[c] = stage.tile([P, 2 * PASS], BF16, name="h%d" % c, tag="hid", align_bytes=64)
             nc.vector.tensor_tensor(
-                hidden[b, g][:, s * PASS : (s + 1) * PASS].rearrange("p (j t) -> p j t", t=PACK),
+                hidden[c][:, b * PASS : (b + 1) * PASS].rearrange("p (j t) -> p j t", t=PACK),
                 bank[:].rearrange("p t j -> p j t"),
                 gates[b, c][:],
                 MULT,
             )
 
-        def quantize_hidden(b, g):
-            pair = quantize(hidden[b, g][:], H_GROUP * CHUNK, "h%d_%d" % (b, g))
-            for s in range(H_GROUP):
-                hq[b, g * H_GROUP + s] = chunk_of(pair, s * CHUNK)
+        def quantize_hidden(c):
+            pair = quantize(hidden[c][:], 2 * CHUNK, "h%d" % c)
+            for b in range(2):
+                hq[b, c] = chunk_of(pair, b * CHUNK)
 
         def prepare(name, b, first, second):
             round_weight((name, 0, b), first)
@@ -206,55 +201,65 @@ def tile_list_silu_noneP_kernel(
         yb = {}
 
         def down(c):
-            q, half = divmod(c, 2)
-            if half == 0:
-                ys[q] = raw.tile([P, PACK, QUARTER], F32, name="y%d" % q, tag="raw")
             bank = product("d", 0, [hq[0, c], hq[1, c]])
-            nc.scalar.copy(ys[q][:, :, half * CHUNK : (half + 1) * CHUNK], bank[:])
+            j0, width = groups[c]
+            if j0 == c * CHUNK:
+                ys[j0] = raw.tile([P, PACK, width], F32, name="y%d" % j0, tag="raw")
+                yb[j0] = stage.tile([P, PACK * width], BF16, name="yb%d" % j0, tag="xbf", bufs=3, align_bytes=64)
+            c0 = c * CHUNK - j0
+            cols = ys[j0][:, :, c0 : c0 + CHUNK]
+            dst = yb[j0][:, c0 * PACK : (c0 + CHUNK) * PACK]
+            nc.scalar.copy(cols, bank[:])
+            if c < CHUNKS - 2:
+                nc.scalar.copy(dst.rearrange("p (j t) -> p j t", t=PACK), bank[:].rearrange("p t j -> p j t"))
+            else:
+                nc.vector.tensor_copy(
+                    dst.rearrange("p (c e t) -> p c t e", e=4, t=PACK), cols.rearrange("p t (c e) -> p c t e", e=4)
+                )
+            if c0 + CHUNK == width:
+                nc.sync.dma_start(y_rows[:, :, j0 : j0 + width], ys[j0][:])
 
-        def round_y(q):
-            cols = slice(q * QUARTER, (q + 1) * QUARTER)
-            nc.sync.dma_start(y_rows[:, :, cols], ys[q][:])
-            yb[q] = stage.tile([P, PACK * QUARTER], BF16, name="yb%d" % q, tag="xbf", bufs=3, align_bytes=64)
-            nc.vector.tensor_copy(
-                yb[q][:].rearrange("p (c e t) -> p c t e", e=4, t=PACK),
-                ys[q][:].rearrange("p t (c e) -> p c t e", e=4),
-            )
+        def quantize_y(c):
+            j0, width = groups[c]
+            if j0 + width == (c + 1) * CHUNK:
+                cols = slice(j0, j0 + width)
+                nc.vector.quantize_mx(out=y_codes[:, cols].bitcast(FP8X4), scales=y_scales[:, cols], in_=yb[j0][:])
+                nc.sync.dma_start(words[:, cols], y_codes[:, cols].bitcast(I32))
 
-        def quantize_y(q):
-            cols = slice(q * QUARTER, (q + 1) * QUARTER)
-            nc.vector.quantize_mx(out=y_codes[:, cols].bitcast(FP8X4), scales=y_scales[:, cols], in_=yb[q][:])
-            nc.sync.dma_start(words[:, cols], y_codes[:, cols].bitcast(I32))
-
-        round_weight(("u", 1, 0), vector_copy)
-        for a in range(2):
-            quantize_weight(("u", a, 0))
+        groups = [
+            (c // 2 * QUARTER, QUARTER) if c < CHUNKS - 0 else (c * CHUNK, CHUNK) for c in range(CHUNKS)
+        ]
+        round_weight(("g", 1, 1), vector_copy)
+        quantize_weight(("g", 1, 1))
         for c in range(CHUNKS):
             gate(0, c)
-        prepare("g", 1, scalar_copy, vector_copy)
-        for c in range(CHUNKS + 1):
+        for c in range(4):
+            gate(1, c)
+        round_weight(("u", 0, 0), vector_copy)
+        quantize_weight(("u", 0, 0))
+        round_weight(("u", 0, 1), vector_copy)
+        quantize_weight(("u", 0, 1))
+        round_weight(("u", 1, 0), vector_copy)
+        quantize_weight(("u", 1, 0))
+        round_weight(("u", 1, 1), vector_copy)
+        quantize_weight(("u", 1, 1))
+        round_weight(("d", 0, 0), scalar_copy)
+        quantize_weight(("d", 0, 0))
+        round_weight(("d", 1, 0), scalar_copy)
+        quantize_weight(("d", 1, 0))
+        for c in range(CHUNKS + 4):
+            if c + 4 < CHUNKS:
+                gate(1, c + 4)
             if c < CHUNKS:
                 up(0, c)
-            if c > 0 and c % H_GROUP == 0:
-                quantize_hidden(0, c // H_GROUP - 1)
-        prepare("u", 1, scalar_copy, vector_copy)
-        prepare("d", 0, scalar_copy, vector_copy)
-        for c in range(CHUNKS):
-            gate(1, c)
-        for q in range(4 + 3):
-            if q < 4:
-                up(1, 2 * q)
-            if 1 <= q < 5:
-                for g in range(2 // H_GROUP):
-                    quantize_hidden(1, (q - 1) * (2 // H_GROUP) + g)
-                down(2 * q - 2)
-                down(2 * q - 1)
-            if q < 4:
-                up(1, 2 * q + 1)
-            if 2 <= q < 6:
-                round_y(q - 2)
-            if 3 <= q:
-                quantize_y(q - 3)
+            if 1 <= c <= CHUNKS:
+                quantize_hidden(c - 1)
+            if c < CHUNKS:
+                up(1, c)
+            if c > 3:
+                quantize_y(c - 4)
+            if 3 <= c < CHUNKS + 3:
+                down(c - 3)
         scale_rows = out_2[0].bitcast(I32)
         for g in range(4):
             nc.scalar.dma_start(scale_rows[4 * g : 4 * g + 4, :], y_scales[32 * g : 32 * g + 4, :].bitcast(I32))

@@ -40,12 +40,12 @@ def tile_list_silu_noneP_kernel(
         psum = ctx.enter_context(tc.psum_pool(name="psum", bufs=8))
 
         offsets = keep.tile([P, J // LIST_ROWS], U16, name="offsets")
-        nc.sync.dma_start(offsets[:], offs)
 
         x_rows = xT.rearrange("(a p i) t -> a i p t", p=P, i=PACK)
         planes = {}
         weights = {}
-        blocks = [(name, w, a, b) for name, w in (("g", wg), ("u", wu)) for a in range(2) for b in range(2)]
+        blocks = [("g", wg, a, b) for a in range(2) for b in range(2)]
+        blocks = blocks + [("u", wu, a, b) for b in range(2) for a in range(2)]
         blocks = blocks + [("d", wd, a, 0) for a in range(2)]
 
         def load_plane(n):
@@ -59,8 +59,9 @@ def tile_list_silu_noneP_kernel(
 
         gain = keep.tile([P, J], F32, name="gain")
         load_plane(0)
-        for j0 in (0, HALF):
-            nc.sync.dma_start(gain[:, j0 : j0 + HALF], wgt[:, j0 : j0 + HALF])
+        nc.sync.dma_start(offsets[:], offs)
+        for j0, j1 in ((0, QUARTER), (QUARTER, J)):
+            nc.sync.dma_start(gain[:, j0:j1], wgt[:, j0:j1])
         early = 0
         for n in range(1, 2 * PACK):
             load_plane(n)
@@ -107,9 +108,9 @@ def tile_list_silu_noneP_kernel(
         def quantize_weight(key):
             wq[key] = quantize(rounded[key][:], PASS, "%s%d%d" % key)
 
-        def round_picked(a, base, j0, width):
+        def round_picked(a, base, j0, width, copy=scalar_copy):
             rounded[a, j0] = stage.tile([P, PACK * width], BF16, name="rx%d_%d" % (a, j0), tag="xbf", bufs=3, align_bytes=64)
-            nc.scalar.copy(
+            copy(
                 rounded[a, j0][:].rearrange("p (c e i) -> p c i e", e=4, i=PACK),
                 picked[a, base][:, :, j0 - base : j0 - base + width].rearrange("p i (c e) -> p c i e", e=4),
             )
@@ -141,7 +142,9 @@ def tile_list_silu_noneP_kernel(
         warm = keep.tile([P, 1], F32, name="warm")
         nc.scalar.activation(warm[:], zero[:], SILU)
 
-        for n in range(PACK):
+        for j0, width in spans[1]:
+            gather(0, j0 // HALF * HALF, j0, width)
+        for n in range(1, PACK):
             for j0, width in halves:
                 gather(n, j0, j0, width)
         for j0, width in halves:
@@ -174,7 +177,7 @@ def tile_list_silu_noneP_kernel(
         def up(b, c):
             bank = product("u", b, [xq[0, c], xq[1, c]])
             if b == 0:
-                hidden[c] = stage.tile([P, 2 * PASS], BF16, name="h%d" % c, tag="hid", align_bytes=64)
+                hidden[c] = stage.tile([P, 2 * PASS], BF16, name="h%d" % c, tag="hid", bufs=7, align_bytes=64)
             nc.vector.tensor_tensor(
                 hidden[c][:, b * PASS : (b + 1) * PASS].rearrange("p (j t) -> p j t", t=PACK),
                 bank[:].rearrange("p t j -> p j t"),
@@ -186,12 +189,6 @@ def tile_list_silu_noneP_kernel(
             pair = quantize(hidden[c][:], 2 * CHUNK, "h%d" % c)
             for b in range(2):
                 hq[b, c] = chunk_of(pair, b * CHUNK)
-
-        def prepare(name, b, first, second):
-            round_weight((name, 0, b), first)
-            round_weight((name, 1, b), second)
-            for a in range(2):
-                quantize_weight((name, a, b))
 
         y_rows = out_0.rearrange("(p t) j -> p t j", t=PACK)
         words = out_1[0].rearrange("p j i -> p (j i)").bitcast(I32)
@@ -210,7 +207,7 @@ def tile_list_silu_noneP_kernel(
             cols = ys[j0][:, :, c0 : c0 + CHUNK]
             dst = yb[j0][:, c0 * PACK : (c0 + CHUNK) * PACK]
             nc.scalar.copy(cols, bank[:])
-            if c < CHUNKS - 2:
+            if c < CHUNKS - 4:
                 nc.scalar.copy(dst.rearrange("p (j t) -> p j t", t=PACK), bank[:].rearrange("p t j -> p j t"))
             else:
                 nc.vector.tensor_copy(
@@ -237,10 +234,12 @@ def tile_list_silu_noneP_kernel(
             gate(1, c)
         round_weight(("u", 0, 0), vector_copy)
         quantize_weight(("u", 0, 0))
-        round_weight(("u", 0, 1), vector_copy)
-        quantize_weight(("u", 0, 1))
         round_weight(("u", 1, 0), vector_copy)
         quantize_weight(("u", 1, 0))
+        for c in range(4):
+            up(0, c)
+        round_weight(("u", 0, 1), vector_copy)
+        quantize_weight(("u", 0, 1))
         round_weight(("u", 1, 1), vector_copy)
         quantize_weight(("u", 1, 1))
         round_weight(("d", 0, 0), scalar_copy)
@@ -250,8 +249,8 @@ def tile_list_silu_noneP_kernel(
         for c in range(CHUNKS + 4):
             if c + 4 < CHUNKS:
                 gate(1, c + 4)
-            if c < CHUNKS:
-                up(0, c)
+            if c + 4 < CHUNKS:
+                up(0, c + 4)
             if 1 <= c <= CHUNKS:
                 quantize_hidden(c - 1)
             if c < CHUNKS:

from contextlib import ExitStack

import concourse.mybir as mybir

K, R, N, T, J = 1024, 1024, 512, 2048, 1024
FLOPS = 2 * (2 * K * R * J + R * N * J)

F32 = mybir.dt.float32
BF16 = mybir.dt.bfloat16
I32 = mybir.dt.int32
U32 = mybir.dt.uint32
U16 = mybir.dt.uint16
U8 = mybir.dt.uint8
FP8X4 = mybir.dt.float8_e4m3fn_x4
MULT = mybir.AluOpType.mult
SILU = mybir.ActivationFunctionType.Silu

P = 128
PACK = 4
PASS = P * PACK
HALF = J // 2
QUARTER = J // 4
CHUNK = 128
CHUNKS = J // CHUNK
LIST_ROWS = 16
H_GROUP = 2


def tile_list_silu_noneP_kernel(
    tc, xT, wgt, wg, wu, wd, offs, out_0, out_1, out_2
):
    nc = tc.nc
    scalar_copy = nc.scalar.copy
    vector_copy = nc.vector.tensor_copy
    with ExitStack() as ctx:
        keep = ctx.enter_context(tc.tile_pool(name="keep", bufs=1))
        raw = ctx.enter_context(tc.tile_pool(name="raw", bufs=9))
        stage = ctx.enter_context(tc.tile_pool(name="stage", bufs=4))
        acts = ctx.enter_context(tc.tile_pool(name="acts", bufs=16))
        psum = ctx.enter_context(tc.psum_pool(name="psum", bufs=8))

        offsets = keep.tile([P, J // LIST_ROWS], U16, name="offsets")

        x_rows = xT.rearrange("(a p i) t -> a i p t", p=P, i=PACK)
        planes = {}
        weights = {}
        blocks = [("g", wg, a, b) for a in range(2) for b in range(2)]
        blocks = blocks + [("u", wu, a, b) for b in range(2) for a in range(2)]
        blocks = blocks + [("d", wd, a, 0) for a in range(2)]

        def load_plane(n):
            planes[n] = raw.tile([P, T], F32, name="plane%d" % n, tag="raw")
            nc.sync.dma_start(planes[n][:], x_rows[n // PACK, n % PACK])

        def load_weight(name, w, a, b):
            weights[name, a, b] = raw.tile([P, PACK, PASS], F32, name="w_%s%d%d" % (name, a, b), tag="raw")
            rows = w[a * PASS : (a + 1) * PASS, b * PASS : (b + 1) * PASS]
            nc.sync.dma_start(weights[name, a, b][:], rows.rearrange("(p i) c -> p i c", i=PACK))

        gain = keep.tile([P, J], F32, name="gain")
        load_plane(0)
        nc.sync.dma_start(offsets[:], offs)
        for j0, j1 in ((0, QUARTER), (QUARTER, J)):
            nc.sync.dma_start(gain[:, j0:j1], wgt[:, j0:j1])
        early = 0
        for n in range(1, 2 * PACK):
            load_plane(n)
            if n in (4, 5, 6):
                load_weight(*blocks[early])
                early = early + 1
        for block in blocks[early:]:
            load_weight(*block)

        halves = ((0, HALF), (HALF, HALF))
        spans = (halves, ((0, QUARTER), (QUARTER, QUARTER), (HALF, HALF)))
        picked = {}
        for a in range(2):
            for j0, width in spans[a]:
                picked[a, j0] = keep.tile([P, PACK, width], F32, name="picked%d_%d" % (a, j0))

        def gather(n, base, j0, width):
            a, i = divmod(n, PACK)
            dst = picked[a, base][:, i, j0 - base : j0 - base + width]
            window = planes[n][:].indirect(offsets[:, j0 // LIST_ROWS : (j0 + width) // LIST_ROWS])
            nc.vector.tensor_tensor(dst, window, gain[:, j0 : j0 + width], MULT)

        def quantize(src, width, name):
            codes = keep.tile([P, width], U32, name="c_" + name, align_bytes=64)
            scales = keep.tile([P, width], U8, name="s_" + name, align_bytes=64)
            nc.vector.quantize_mx(out=codes[:].bitcast(FP8X4), scales=scales[:], in_=src)
            return codes, scales

        def chunk_of(pair, c0):
            return pair[0][:, c0 : c0 + CHUNK], pair[1][:, c0 : c0 + CHUNK]

        rounded = {}
        wq = {}
        xq = {}
        hq = {}

        def round_weight(key, copy):
            rounded[key] = stage.tile([P, PACK * PASS], BF16, name="r_%s%d%d" % key, tag="wbf", align_bytes=64)
            copy(
                rounded[key][:].rearrange("p (t m i) -> p m i t", t=PACK, i=PACK),
                weights[key][:].rearrange("p i (m t) -> p m i t", t=PACK),
            )

        def quantize_weight(key):
            wq[key] = quantize(rounded[key][:], PASS, "%s%d%d" % key)

        def round_picked(a, base, j0, width, copy=scalar_copy):
            rounded[a, j0] = stage.tile([P, PACK * width], BF16, name="rx%d_%d" % (a, j0), tag="xbf", bufs=3, align_bytes=64)
            copy(
                rounded[a, j0][:].rearrange("p (c e i) -> p c i e", e=4, i=PACK),
                picked[a, base][:, :, j0 - base : j0 - base + width].rearrange("p i (c e) -> p c i e", e=4),
            )

        def quantize_picked(a, j0, width):
            pair = quantize(rounded[a, j0][:], width, "x%d_%d" % (a, j0))
            for c0 in range(0, width, CHUNK):
                xq[a, (j0 + c0) // CHUNK] = chunk_of(pair, c0)

        def product(name, b, moving):
            bank = psum.tile([P, PACK, CHUNK], F32, name="bank")
            for a in range(2):
                codes, scales = wq[name, a, b]
                for t in range(PACK):
                    cols = slice(t * P, (t + 1) * P)
                    nc.tensor.matmul_mx(
                        out=bank[:, t, :],
                        lhsT=codes[:, cols].bitcast(FP8X4),
                        lhsT_scale=scales[:, cols],
                        rhs=moving[a][0].bitcast(FP8X4),
                        rhs_scale=moving[a][1],
                        start=(a == 0 and t == 0),
                        stop=(a == 1 and t == PACK - 1),
                    )
            return bank

        zero = keep.tile([P, 1], F32, name="zero")
        nc.vector.memset(zero[:], 0.0)
        warm = keep.tile([P, 1], F32, name="warm")
        nc.scalar.activation(warm[:], zero[:], SILU)

        for j0, width in spans[1]:
            gather(0, j0 // HALF * HALF, j0, width)
        for n in range(1, PACK):
            for j0, width in halves:
                gather(n, j0, j0, width)
        for j0, width in halves:
            round_picked(0, j0, j0, width)
        round_weight(("g", 0, 0), scalar_copy)
        round_weight(("g", 0, 1), scalar_copy)
        round_weight(("g", 1, 0), scalar_copy)
        for n in range(PACK, 2 * PACK - 1):
            for j0, width in spans[1]:
                gather(n, j0, j0, width)
        for j0, width in halves:
            quantize_picked(0, j0, width)
        quantize_weight(("g", 0, 0))
        quantize_weight(("g", 0, 1))
        quantize_weight(("g", 1, 0))
        for j0, width in spans[1]:
            gather(2 * PACK - 1, j0, j0, width)
            round_picked(1, j0, j0, width)
        for j0, width in spans[1]:
            quantize_picked(1, j0, width)

        gates = {}
        hidden = {}

        def gate(b, c):
            bank = product("g", b, [xq[0, c], xq[1, c]])
            gates[b, c] = acts.tile([P, CHUNK, PACK], F32, name="gate%d_%d" % (b, c), tag="gate")
            nc.scalar.activation(gates[b, c][:], bank[:].rearrange("p t j -> p j t"), SILU)

        def up(b, c):
            bank = product("u", b, [xq[0, c], xq[1, c]])
            if b == 0:
                hidden[c] = stage.tile([P, 2 * PASS], BF16, name="h%d" % c, tag="hid", bufs=7, align_bytes=64)
            nc.vector.tensor_tensor(
                hidden[c][:, b * PASS : (b + 1) * PASS].rearrange("p (j t) -> p j t", t=PACK),
                bank[:].rearrange("p t j -> p j t"),
                gates[b, c][:],
                MULT,
            )

        def quantize_hidden(c):
            pair = quantize(hidden[c][:], 2 * CHUNK, "h%d" % c)
            for b in range(2):
                hq[b, c] = chunk_of(pair, b * CHUNK)

        y_rows = out_0.rearrange("(p t) j -> p t j", t=PACK)
        words = out_1[0].rearrange("p j i -> p (j i)").bitcast(I32)
        y_codes = keep.tile([P, J], U32, name="y_codes", align_bytes=64)
        y_scales = keep.tile([P, J], U8, name="y_scales", align_bytes=64)
        ys = {}
        yb = {}

        def down(c):
            bank = product("d", 0, [hq[0, c], hq[1, c]])
            j0, width = groups[c]
            if j0 == c * CHUNK:
                ys[j0] = raw.tile([P, PACK, width], F32, name="y%d" % j0, tag="raw")
                yb[j0] = stage.tile([P, PACK * width], BF16, name="yb%d" % j0, tag="xbf", bufs=3, align_bytes=64)
            c0 = c * CHUNK - j0
            cols = ys[j0][:, :, c0 : c0 + CHUNK]
            dst = yb[j0][:, c0 * PACK : (c0 + CHUNK) * PACK]
            nc.scalar.copy(cols, bank[:])
            if c < CHUNKS - 4:
                nc.scalar.copy(dst.rearrange("p (j t) -> p j t", t=PACK), bank[:].rearrange("p t j -> p j t"))
            else:
                nc.vector.tensor_copy(
                    dst.rearrange("p (c e t) -> p c t e", e=4, t=PACK), cols.rearrange("p t (c e) -> p c t e", e=4)
                )
            if c0 + CHUNK == width:
                nc.sync.dma_start(y_rows[:, :, j0 : j0 + width], ys[j0][:])

        def quantize_y(c):
            j0, width = groups[c]
            if j0 + width == (c + 1) * CHUNK:
                cols = slice(j0, j0 + width)
                nc.vector.quantize_mx(out=y_codes[:, cols].bitcast(FP8X4), scales=y_scales[:, cols], in_=yb[j0][:])
                nc.sync.dma_start(words[:, cols], y_codes[:, cols].bitcast(I32))

        groups = [
            (c // 2 * QUARTER, QUARTER) if c < CHUNKS - 0 else (c * CHUNK, CHUNK) for c in range(CHUNKS)
        ]
        round_weight(("g", 1, 1), vector_copy)
        quantize_weight(("g", 1, 1))
        for c in range(CHUNKS):
            gate(0, c)
        for c in range(4):
            gate(1, c)
        round_weight(("u", 0, 0), vector_copy)
        quantize_weight(("u", 0, 0))
        round_weight(("u", 1, 0), vector_copy)
        quantize_weight(("u", 1, 0))
        for c in range(4):
            up(0, c)
        round_weight(("u", 0, 1), vector_copy)
        quantize_weight(("u", 0, 1))
        round_weight(("u", 1, 1), vector_copy)
        quantize_weight(("u", 1, 1))
        round_weight(("d", 0, 0), scalar_copy)
        quantize_weight(("d", 0, 0))
        round_weight(("d", 1, 0), scalar_copy)
        quantize_weight(("d", 1, 0))
        for c in range(CHUNKS + 4):
            if c + 4 < CHUNKS:
                gate(1, c + 4)
            if c + 4 < CHUNKS:
                up(0, c + 4)
            if 1 <= c <= CHUNKS:
                quantize_hidden(c - 1)
            if c < CHUNKS:
                up(1, c)
            if c > 3:
                quantize_y(c - 4)
            if 3 <= c < CHUNKS + 3:
                down(c - 3)
        scale_rows = out_2[0].bitcast(I32)
        for g in range(4):
            nc.scalar.dma_start(scale_rows[4 * g : 4 * g + 4, :], y_scales[32 * g : 32 * g + 4, :].bitcast(I32))
